import numpy as np
import ml_dtypes


def mxq(x, axis, fmt="e4m3"):
    dtype, down = {"e4m3": (ml_dtypes.float8_e4m3fn, 7), "e5m2": (ml_dtypes.float8_e5m2, 14)}[fmt]
    v = np.moveaxis(np.asarray(x, np.float32).astype(ml_dtypes.bfloat16).astype(np.float64), axis, -1)
    blocks = v.reshape(v.shape[:-1] + (-1, 32))
    amax = np.abs(blocks).max(-1, keepdims=True)
    byte = np.maximum(np.where(amax > 0, np.frexp(amax)[1] - 1 + 127, 0) - down, 1)
    scale = np.exp2(byte - 127.0)
    codes = (blocks / scale).astype(np.float32).astype(dtype).astype(np.float64)
    return np.moveaxis((codes * scale).reshape(v.shape), -1, axis)


WIDE = False


def mx_kscale(k):
    if not WIDE:
        return np.ones(k)
    levels = np.array([10, -10, 5, -5, 0])
    if k % 512:
        return np.exp2(np.random.permutation(np.resize(levels, k // 32))).repeat(32)
    a = np.empty((k // 512, 16))
    for p in range(k // 512):
        a[p, :8] = np.random.permutation(np.resize(levels, 8))
        for g in range(8):
            far = levels[np.abs(levels - a[p, g]) >= 10]
            a[p, g + 8] = far[np.random.randint(len(far))]
    return np.exp2(a.ravel()).repeat(32)


BF16 = ml_dtypes.bfloat16


def bf(x):
    return np.asarray(x, np.float32).astype(BF16)


def f64(x):
    return np.asarray(x).astype(np.float64)


E2M1 = np.array([0.0, 0.5, 1.0, 1.5, 2.0, 3.0, 4.0, 6.0, -0.0, -0.5, -1.0, -1.5, -2.0, -3.0, -4.0, -6.0])


def pack_weight(w, fmt):
    k, n = w.shape
    w = f64(bf(w)).reshape(k // 32, 32, n)
    amax = np.abs(w).max(1)
    if fmt == "e4m3":
        byte = np.frexp(amax)[1] - 1 + 127 - 7
    else:
        mant, ex = np.frexp(amax / 6.0)
        byte = np.where(mant > 0.5, ex, ex - 1) + 127
    byte = np.clip(np.where(amax > 0, byte, 1), 1, 254)
    scaled = (w * np.exp2(127.0 - byte)[:, None, :]).reshape(k, n).astype(np.float32)
    by_word = np.ascontiguousarray(scaled.reshape(k // 512, 128, 4, n).transpose(0, 1, 3, 2))
    if fmt == "e4m3":
        words = by_word.astype(ml_dtypes.float8_e4m3fn).view(np.uint8)
    else:
        c = by_word.astype(ml_dtypes.float4_e2m1fn).view(np.uint8) & 0xF
        words = c[..., 0::2] | (c[..., 1::2] << 4)
    return np.ascontiguousarray(words), np.ascontiguousarray(byte.astype(np.uint8).reshape(k // 512, 16, n))


def unpack_weight(words, scales, fmt):
    g, p, n, _ = words.shape
    if fmt == "e4m3":
        vals = np.ascontiguousarray(words).view(ml_dtypes.float8_e4m3fn).astype(np.float64)
    else:
        nib = np.empty((g, p, n, 4), np.uint8)
        nib[..., 0::2] = words & 0xF
        nib[..., 1::2] = words >> 4
        vals = E2M1[nib]
    vals = vals * np.repeat(np.exp2(scales.astype(np.float64) - 127.0), 8, axis=1)[..., None]
    return vals.transpose(0, 1, 3, 2).reshape(g * 512, n)
def pack4(w):
    words, scales = pack_weight(w, "e2m1")
    return words.reshape(words.shape[0], 128, -1), scales


def unpack4(words, scales):
    return unpack_weight(words.reshape(words.shape[0], 128, -1, 2), scales, "e2m1")


E4M3FN = np.array([(-1.0 if i & 128 else 1.0) * ((1.0 + (i & 7) / 8.0) * 2.0 ** (((i >> 3) & 15) - 7) if i & 120 else (i & 7) * 2.0 ** -9) for i in range(256)])


def e4m3fn_bytes(y):
    return np.clip(np.asarray(y, np.float64), -448.0, 448.0).astype(np.float32).astype(ml_dtypes.float8_e4m3fn).view(np.uint8)


def e4m3fn_values(b):
    return E4M3FN[b]

def planes(Y):
    n, m = Y.shape
    b = f64(bf(Y)).reshape(n // 32, 32, m)
    amax = np.abs(b).max(1)
    byte = np.clip(np.where(amax > 0, np.frexp(amax)[1] - 1 + 127 - 7, 1), 1, 254)
    codes = (b * np.exp2(127.0 - byte)[:, None, :]).reshape(n, m).astype(np.float32).astype(ml_dtypes.float8_e4m3fn).view(np.uint8)
    words = codes.reshape(n // 512, 128, 4, m).transpose(0, 1, 3, 2)
    return np.ascontiguousarray(words), np.ascontiguousarray(byte.astype(np.uint8).reshape(n // 512, 16, m))


G, T, K, F, N, B = 3, 512, 1024, 1024, 512, 128

def setup_inputs():
    s = mx_kscale(G * K)
    t = mx_kscale(G * F)
    xq = np.random.randn(G, T, K) * s.reshape(G, 1, K)
    xd = np.random.randn(G, T, K) * s.reshape(G, 1, K)
    xq_scale = (np.abs(xq).reshape(G, T, K // B, B).max(axis=3) / 448.0).astype(np.float32)
    xd_scale = (np.abs(xd).reshape(G, T, K // B, B).max(axis=3) / 448.0).astype(np.float32)
    xq_bytes = e4m3fn_bytes(xq / np.repeat(f64(xq_scale), B, axis=2))
    xd_bytes = e4m3fn_bytes(xd / np.repeat(f64(xd_scale), B, axis=2))
    W1 = np.random.randn(G * K, F) / np.sqrt(K) / s[:, None] * np.repeat(t.reshape(G, F), K, axis=0)
    spread = np.exp(0.8 * np.random.randn(G, N))
    W2 = np.random.randn(G * F, N) / np.sqrt(F) * np.repeat(spread, F, axis=0) / t[:, None]
    w1_words, w1_scales = pack4(W1)
    w2_words, w2_scales = pack4(W2)
    return {"xq_bytes": xq_bytes, "xq_scale": xq_scale, "xd_bytes": xd_bytes, "xd_scale": xd_scale,
            "w1_words": w1_words, "w1_scales": w1_scales, "w2_words": w2_words, "w2_scales": w2_scales,
            "bias": bf(0.3 * spread * np.random.randn(G, N)), "prior": bf(np.random.randn(G, T))}

def reference(xq_bytes, xq_scale, xd_bytes, xd_scale, w1_words, w1_scales, w2_words, w2_scales, bias, prior):
    xq = e4m3fn_values(xq_bytes) * np.repeat(f64(xq_scale), B, axis=2)
    xd = e4m3fn_values(xd_bytes) * np.repeat(f64(xd_scale), B, axis=2)
    W1 = unpack4(w1_words, w1_scales).reshape(G, K, F)
    W2 = unpack4(w2_words, w2_scales).reshape(G, F, N)
    hq = mxq(xq, 2, "e4m3") @ W1
    hd = mxq(xd, 2, "e4m3") @ W1
    z = np.abs(hq - hd)
    rel = (mxq(z, 2, "e4m3") @ W2) + f64(bias)[:, None, :]
    gate = 1.0 / (1.0 + np.exp(-f64(prior)))
    y = rel * gate[:, :, None]
    Y = y.reshape(G * T, N).T
    words, scales = planes(Y)
    return y, words, scales

@@ -1,0 +1,407 @@
+from contextlib import ExitStack
+
+import concourse.mybir as mybir
+from concourse.masks import make_identity
+
+G, T, K, F, N, B = 3, 512, 1024, 1024, 512, 128
+FLOPS = 2 * G * T * (2 * K * F + F * N)
+
+F32 = mybir.dt.float32
+BF16 = mybir.dt.bfloat16
+I32 = mybir.dt.int32
+U32 = mybir.dt.uint32
+U8 = mybir.dt.uint8
+FP8 = mybir.dt.float8_e4m3fn
+FP8X4 = mybir.dt.float8_e4m3fn_x4
+FP4X4 = mybir.dt.float4_e2m1fn_x4
+ACT = mybir.ActivationFunctionType
+ALU = mybir.AluOpType
+
+P = 128
+PASS = 512
+PASSES = K // PASS
+TILES_PER_FIELD = T // P
+TILES = G * TILES_PER_FIELD
+BLOCKS = K // B
+BLOCKS_PER_PASS = PASS // B
+SIDES = 2
+BOTH = tuple(range(PASSES))
+
+
+def tile_siamese_field_rerank_b12_kernel(
+    tc, xq_bytes, xq_scale, xd_bytes, xd_scale, w1_words, w1_scales, w2_words, w2_scales, bias, prior,
+    out_0, out_1, out_2,
+):
+    nc = tc.nc
+    x_bytes = (xq_bytes, xd_bytes)
+    x_scale = (xq_scale, xd_scale)
+
+    with ExitStack() as ctx:
+        keep = ctx.enter_context(tc.tile_pool(name="keep", bufs=1))
+        work = ctx.enter_context(tc.tile_pool(name="work", bufs=2))
+        psum = ctx.enter_context(tc.psum_pool(name="psum", bufs=1))
+        ctx.enter_context(tc.manual_schedule())
+
+        raw, row_scale, w1, w1_plane, w2 = {}, {}, {}, {}, {}
+
+        def load_bytes(side, first, count):
+            name = "fp8_in_%d_%d" % (side, first)
+            held = keep.tile([P, count, K], U8, name=name, tag=name)
+            rows = x_bytes[side].rearrange("i (j p) k -> p (i j) k", p=P)
+            nc.sync.dma_start(out=held[:], in_=rows[:, first : first + count, :])
+            for j in range(count):
+                raw[side, first + j] = held[:, j, :]
+
+        def load_row_scales(side, first, count):
+            name = "row_scale_%d_%d" % (side, first)
+            held = keep.tile([P, count, BLOCKS], F32, name=name, tag=name)
+            rows = x_scale[side].rearrange("i (j p) b -> p (i j) b", p=P)
+            nc.sync.dma_start(out=held[:], in_=rows[:, first : first + count, :])
+            return held
+
+        def use_row_scales(side, first, count, held):
+            if side == 1:
+                name = "negated_scale_%d" % first
+                negated = keep.tile([P, count, BLOCKS], F32, name=name, tag=name)
+                nc.vector.tensor_scalar(out=negated[:], in0=held[:], scalar1=-1.0, scalar2=None, op0=ALU.mult)
+                held = negated
+            for j in range(count):
+                row_scale[side, first + j] = held[:, j, :]
+
+        def load_words(store, words, label, first, count):
+            name = "%s_words_%d" % (label, first)
+            held = keep.tile([P, count, words.shape[2]], U8, name=name, tag=name, align_bytes=64)
+            nc.sync.dma_start(
+                out=held[:].bitcast(I32),
+                in_=words[first : first + count].rearrange("g p n -> p g n").bitcast(I32),
+            )
+            for g in range(count):
+                store[first + g] = held[:, g, :]
+
+        def new_plane(engine, label, count, width):
+            plane = keep.tile([P, count, width], U8, name=label, tag=label, align_bytes=64)
+            engine.memset(plane[:].bitcast(I32), 0)
+            return plane
+
+        def load_plane(plane, scales, first, count):
+            for q in range(4):
+                nc.sync.dma_start(
+                    out=plane[32 * q : 32 * q + 4, :, :].bitcast(I32),
+                    in_=scales[first : first + count, 4 * q : 4 * q + 4, :].rearrange("g r n -> r g n").bitcast(I32),
+                )
+
+        prior_rows = keep.tile([TILES, P], BF16, name="prior_rows")
+        nc.gpsimd.dma_start(out=prior_rows[:], in_=prior.rearrange("i (j p) -> (i j) p", p=P))
+        identity = keep.tile([P, P], F32, name="identity")
+        make_identity(nc, identity[:])
+        gate_rows = keep.tile([P, P], F32, name="gate_rows")
+        nc.gpsimd.memset(gate_rows[:], 0.0)
+        w1_plane_first = new_plane(nc.vector, "w1_plane_first", PASSES, F)
+        w2_plane = new_plane(nc.vector, "w2_plane", G * PASSES, N)
+        w1_plane_rest = new_plane(nc.vector, "w1_plane_rest", (G - 1) * PASSES, F)
+        for g in range(G * PASSES):
+            w1_plane[g] = w1_plane_first[:, g, :] if g < PASSES else w1_plane_rest[:, g - PASSES, :]
+
+        first_scale_q = load_row_scales(0, 0, TILES_PER_FIELD)
+        load_bytes(0, 0, 1)
+        first_scale_d = load_row_scales(1, 0, TILES_PER_FIELD)
+        load_bytes(1, 0, 1)
+        load_plane(w1_plane_first, w1_scales, 0, PASSES)
+        load_words(w1, w1_words, "w1", 0, 1)
+        load_words(w1, w1_words, "w1", 1, 1)
+        load_bytes(0, 1, 1)
+        load_bytes(1, 1, 1)
+        load_bytes(0, 2, 2)
+        load_bytes(1, 2, 2)
+        bias_all = keep.tile([P, G * N], BF16, name="bias_all")
+        nc.sync.dma_start(out=bias_all[:], in_=bias.rearrange("i c -> (i c)").partition_broadcast(P))
+        load_plane(w2_plane, w2_scales, 0, G * PASSES)
+        load_words(w2, w2_words, "w2", 0, PASSES)
+        rest = TILES - TILES_PER_FIELD
+        rest_scale_q = load_row_scales(0, TILES_PER_FIELD, rest)
+        rest_scale_d = load_row_scales(1, TILES_PER_FIELD, rest)
+        load_bytes(0, TILES_PER_FIELD, TILES_PER_FIELD)
+        load_bytes(1, TILES_PER_FIELD, TILES_PER_FIELD)
+        load_plane(w1_plane_rest, w1_scales, PASSES, (G - 1) * PASSES)
+        load_words(w1, w1_words, "w1", PASSES, PASSES)
+        load_words(w2, w2_words, "w2", PASSES, (G - 1) * PASSES)
+        load_bytes(0, 2 * TILES_PER_FIELD, TILES_PER_FIELD)
+        load_bytes(1, 2 * TILES_PER_FIELD, TILES_PER_FIELD)
+        load_words(w1, w1_words, "w1", 2 * PASSES, PASSES)
+
+        nc.scalar.activation(out=gate_rows[0:TILES, :], in_=prior_rows[:], func=ACT.Sigmoid)
+
+        y_codes = keep.tile([P, TILES * P], U32, name="y_codes", align_bytes=64)
+        y_plane = keep.tile([P, TILES * P], U8, name="y_plane", align_bytes=64)
+        gate = keep.tile([P, TILES], F32, name="gate")
+        live = {}
+
+        def make_gate():
+            bank = psum.tile([P, P], F32, name="gate_bank", tag="gate_bank")
+            nc.tensor.transpose(bank[:], gate_rows[:], identity[:])
+            nc.scalar.copy(out=gate[:], in_=bank[:, 0:TILES])
+
+        def widen(t, side, passes=BOTH):
+            for g in passes:
+                name = "x_wide_%d_%d" % (side, g)
+                wide = work.tile([P, PASS], BF16, name=name, tag=name, bufs=3, align_bytes=64)
+                sorted_view = wide[:].rearrange("r (u q p e) -> r q p u e", u=2, q=BLOCKS_PER_PASS, e=2)
+                for q in range(BLOCKS_PER_PASS):
+                    b = g * BLOCKS_PER_PASS + q
+                    codes = raw[side, t][:, b * B : (b + 1) * B].bitcast(FP8)
+                    nc.vector.tensor_scalar(
+                        out=sorted_view[:, q],
+                        in0=codes.rearrange("r (p u e) -> r p u e", u=2, e=2),
+                        scalar1=row_scale[side, t][:, b : b + 1],
+                        scalar2=None,
+                        op0=ALU.mult,
+                    )
+                live["x_wide", t, side, g] = wide
+
+        def turn(label, sources):
+            bank = psum.tile([P, 2 * len(sources), P], F32, name=label, tag=label)
+            for g, source in enumerate(sources):
+                words = source[:].bitcast(F32)
+                for u in range(2):
+                    nc.tensor.transpose(bank[:, 2 * g + u, :], words[:, u * P : (u + 1) * P], identity[:])
+            return bank
+
+        def gather(label, bank):
+            passes = bank.shape[1] // 2
+            grouped = work.tile([P, passes * PASS], BF16, name=label, tag=label, align_bytes=64)
+            nc.scalar.copy(
+                out=grouped[:].bitcast(F32).rearrange("p (g r u) -> p g r u", g=passes, u=2),
+                in_=bank[:].rearrange("p (g u) r -> p g r u", u=2),
+            )
+            return grouped
+
+        def quantize(label, grouped):
+            passes = grouped.shape[1] // PASS
+            codes = work.tile([P, passes * P], U32, name=label + "_codes", tag=label + "_codes", bufs=3, align_bytes=64)
+            plane = work.tile([P, passes * P], U8, name=label + "_plane", tag=label + "_plane", bufs=3, align_bytes=64)
+            nc.vector.quantize_mx(out=codes[:].bitcast(FP8X4), scales=plane[:], in_=grouped[:])
+            return [(codes[:, g * P : (g + 1) * P], plane[:, g * P : (g + 1) * P]) for g in range(passes)]
+
+        def turn_x(t, side, passes=BOTH, bank=None):
+            sources = [live["x_wide", t, side, g] for g in passes]
+            live["x_bank", t, side, passes] = turn(bank or "x_bank_%d" % side, sources)
+
+        def gather_x(t, side, passes=BOTH):
+            live["x_grouped", t, side, passes] = gather("x_grouped_%d" % side, live["x_bank", t, side, passes])
+
+        def quantize_x(t, side, passes=BOTH):
+            for g, pair in zip(passes, quantize("x_mx_%d" % side, live["x_grouped", t, side, passes])):
+                live["x_mx", t, side, g] = pair
+
+        def project(t, h, side, passes=BOTH):
+            for g in passes:
+                first = side == 0 and g == 0
+                if first:
+                    name = "diff_bank_%d" % h
+                    live["diff_bank", t, h] = psum.tile([P, PASS], F32, name=name, tag=name)
+                codes, plane = live["x_mx", t, side, g]
+                group = t // TILES_PER_FIELD * PASSES + g
+                nc.tensor.matmul_mx(
+                    out=live["diff_bank", t, h][:],
+                    lhsT=codes.bitcast(FP8X4),
+                    lhsT_scale=plane,
+                    rhs=w1[group][:, 2 * h * PASS : 2 * (h + 1) * PASS].bitcast(FP4X4),
+                    rhs_scale=w1_plane[group][:, h * PASS : (h + 1) * PASS],
+                    start=first,
+                    stop=(side == SIDES - 1 and g == PASSES - 1),
+                )
+
+        def absolute(t, h):
+            name = "z_sorted_%d" % h
+            z = work.tile([P, PASS], BF16, name=name, tag=name, bufs=3, align_bytes=64)
+            nc.scalar.activation(
+                out=z[:].rearrange("r (u p e) -> r u p e", u=2, e=2),
+                in_=live["diff_bank", t, h][:].rearrange("r (p u e) -> r u p e", u=2, e=2),
+                func=ACT.Abs,
+            )
+            live["z_sorted", t, h] = z
+
+        def turn_z(t, passes=BOTH, bank="z_bank"):
+            live["z_bank", t, passes] = turn(bank, [live["z_sorted", t, g] for g in passes])
+
+        def gather_z(t, passes=BOTH):
+            live["z_grouped", t, passes] = gather("z_grouped", live["z_bank", t, passes])
+
+        def quantize_z(t, passes=BOTH):
+            for g, pair in zip(passes, quantize("z_mx", live["z_grouped", t, passes])):
+                live["z_mx", t, g] = pair
+
+        def relevance(t, passes=BOTH, bank="rel_bank"):
+            for g in passes:
+                if g == 0:
+                    live["rel_bank", t] = psum.tile([P, N], F32, name=bank, tag=bank)
+                codes, plane = live["z_mx", t, g]
+                group = t // TILES_PER_FIELD * PASSES + g
+                nc.tensor.matmul_mx(
+                    out=live["rel_bank", t][:],
+                    lhsT=codes.bitcast(FP8X4),
+                    lhsT_scale=plane,
+                    rhs=w2[group].bitcast(FP4X4),
+                    rhs_scale=w2_plane[:, group, :],
+                    start=(g == 0),
+                    stop=(g == PASSES - 1),
+                )
+
+        def gate_bias(t):
+            field = t // TILES_PER_FIELD
+            gated = work.tile([P, N], F32, name="gated_bias", tag="gated_bias", bufs=3)
+            nc.scalar.activation(
+                out=gated[:], in_=bias_all[:, field * N : (field + 1) * N], func=ACT.Copy, scale=gate[:, t : t + 1]
+            )
+            live["gated_bias", t] = gated
+
+        y_rows = out_0.rearrange("i r c -> (i r) c")
+        code_rows = out_1[0].rearrange("p m t -> p (m t)").bitcast(I32)
+
+        def finish(t):
+            y = work.tile([P, N], F32, name="y", tag="y", bufs=3)
+            nc.vector.scalar_tensor_tensor(
+                out=y[:], in0=live["rel_bank", t][:], scalar=gate[:, t : t + 1], in1=live["gated_bias", t][:],
+                op0=ALU.mult, op1=ALU.add,
+            )
+            nc.sync.dma_start(out=y_rows[t * P : (t + 1) * P, :], in_=y[:])
+            live["y", t] = y
+
+        def round_y(t):
+            rounded = work.tile([P, N], BF16, name="y_sorted", tag="y_sorted", align_bytes=64)
+            nc.vector.tensor_copy(
+                out=rounded[:].rearrange("r (u p e) -> r u p e", u=2, e=2),
+                in_=live["y", t][:].rearrange("r (p u e) -> r u p e", u=2, e=2),
+            )
+            live["y_sorted", t] = rounded
+
+        def turn_y(t, bank="y_bank"):
+            live["y_bank", t] = turn(bank, [live["y_sorted", t]])
+
+        def gather_y(t):
+            live["y_grouped", t] = gather("y_grouped", live["y_bank", t])
+
+        def quantize_y(t):
+            cols = slice(t * P, (t + 1) * P)
+            nc.vector.quantize_mx(
+                out=y_codes[:, cols].bitcast(FP8X4), scales=y_plane[:, cols], in_=live["y_grouped", t][:]
+            )
+            nc.sync.dma_start(out=code_rows[:, cols], in_=y_codes[:, cols].bitcast(I32))
+
+        def at(stage, t, *more):
+            if 0 <= t < TILES:
+                stage(t, *more)
+
+        use_row_scales(0, 0, TILES_PER_FIELD, first_scale_q)
+        widen(0, 0)
+        use_row_scales(1, 0, TILES_PER_FIELD, first_scale_d)
+        widen(0, 1)
+        turn_x(0, 0, (0,))
+        turn_x(0, 0, (1,), "z_bank")
+        turn_x(0, 1)
+        gather_x(0, 0, (0,))
+        gather_x(0, 0, (1,))
+        gather_x(0, 1)
+        quantize_x(0, 0, (0,))
+        quantize_x(0, 0, (1,))
+        project(0, 0, 0, (0,))
+        project(0, 1, 0, (0,))
+        project(0, 0, 0, (1,))
+        project(0, 1, 0, (1,))
+        widen(1, 0, (0,))
+        quantize_x(0, 1)
+        widen(1, 0, (1,))
+        widen(1, 1)
+        make_gate()
+        turn_x(1, 0)
+        turn_x(1, 1)
+        project(0, 0, 1)
+        project(0, 1, 1)
+        gather_x(1, 0)
+        gather_x(1, 1)
+        widen(2, 0)
+        widen(2, 1)
+        quantize_x(1, 0)
+        quantize_x(1, 1)
+        absolute(0, 0)
+        gate_bias(0)
+        use_row_scales(0, TILES_PER_FIELD, rest, rest_scale_q)
+
+        last = TILES - 1
+        for s in range(1, last):
+            at(round_y, s - 3)
+            at(turn_z, s - 2)
+            at(turn_x, s + 1, 0)
+            at(turn_x, s + 1, 1)
+            at(turn_y, s - 3)
+            at(widen, s + 2, 0)
+            at(gather_z, s - 2)
+            at(absolute, s - 1, 1)
+            at(quantize_z, s - 2)
+            at(gather_x, s + 1, 0)
+            at(gather_x, s + 1, 1)
+            at(gather_y, s - 3)
+            if s + 2 == TILES_PER_FIELD:
+                use_row_scales(1, TILES_PER_FIELD, rest, rest_scale_d)
+            at(widen, s + 2, 1)
+            at(quantize_x, s + 1, 0)
+            at(quantize_x, s + 1, 1)
+            at(quantize_y, s - 3)
+            at(project, s, 0, 0)
+            at(project, s, 0, 1)
+            at(relevance, s - 2)
+            at(project, s, 1, 0)
+            at(project, s, 1, 1)
+            at(absolute, s, 0)
+            at(gate_bias, s)
+            at(finish, s - 2)
+
+        absolute(last - 1, 1)
+        round_y(last - 3)
+        turn_z(last - 2)
+        turn_y(last - 3)
+        turn_z(last - 1, BOTH, "x_bank_0")
+        gather_z(last - 2)
+        quantize_z(last - 2)
+        gather_z(last - 1)
+        quantize_z(last - 1)
+        gather_y(last - 3)
+        quantize_y(last - 3)
+        project(last, 0, 0)
+        project(last, 0, 1)
+        relevance(last - 2)
+        project(last, 1, 0)
+        project(last, 1, 1)
+        relevance(last - 1, BOTH, "x_bank_1")
+        absolute(last, 0)
+        gate_bias(last)
+        finish(last - 2)
+        round_y(last - 2)
+        absolute(last, 1)
+        turn_z(last, (0,))
+        turn_y(last - 2)
+        turn_z(last, (1,), "x_bank_0")
+        finish(last - 1)
+        gather_z(last, (0,))
+        gather_z(last, (1,))
+        quantize_z(last, (0,))
+        round_y(last - 1)
+        quantize_z(last, (1,))
+        relevance(last)
+        turn_y(last - 1, "gate_bank")
+        gather_y(last - 2)
+        quantize_y(last - 2)
+        gather_y(last - 1)
+        finish(last)
+        round_y(last)
+        quantize_y(last - 1)
+        turn_y(last)
+        gather_y(last)
+        quantize_y(last)
+
+        for q in range(4):
+            queue = nc.scalar if q % 2 else nc.sync
+            queue.dma_start(
+                out=out_2[0, 4 * q : 4 * q + 4, :].bitcast(I32),
+                in_=y_plane[32 * q : 32 * q + 4, :].bitcast(I32),
+            )

@@ -25,6 +25,7 @@ TILES = G * TILES_PER_FIELD
 BLOCKS = K // B
 BLOCKS_PER_PASS = PASS // B
 SIDES = 2
+PRESORTED = ((1, 0), (1, 1))
 BOTH = tuple(range(PASSES))
 
 
@@ -141,29 +142,34 @@ def tile_siamese_field_rerank_b12_kernel(
             nc.tensor.transpose(bank[:], gate_rows[:], identity[:])
             nc.scalar.copy(out=gate[:], in_=bank[:, 0:TILES])
 
+        def halves(tile):
+            words = tile[:].bitcast(F32)
+            return [words[:, u * P : (u + 1) * P] for u in range(2)]
+
         def widen(t, side, passes=BOTH):
             for g in passes:
                 name = "x_wide_%d_%d" % (side, g)
                 wide = work.tile([P, PASS], BF16, name=name, tag=name, bufs=3, align_bytes=64)
                 sorted_view = wide[:].rearrange("r (u q p e) -> r q p u e", u=2, q=BLOCKS_PER_PASS, e=2)
+                presorted = (side, g) in PRESORTED
                 for q in range(BLOCKS_PER_PASS):
                     b = g * BLOCKS_PER_PASS + q
                     codes = raw[side, t][:, b * B : (b + 1) * B].bitcast(FP8)
                     nc.vector.tensor_scalar(
-                        out=sorted_view[:, q],
-                        in0=codes.rearrange("r (p u e) -> r p u e", u=2, e=2),
+                        out=sorted_view[:, q] if presorted else wide[:, q * B : (q + 1) * B],
+                        in0=codes.rearrange("r (p u e) -> r p u e", u=2, e=2) if presorted else codes,
                         scalar1=row_scale[side, t][:, b : b + 1],
                         scalar2=None,
                         op0=ALU.mult,
                     )
-                live["x_wide", t, side, g] = wide
+                words = wide[:].bitcast(F32)
+                live["x_wide", t, side, g] = halves(wide) if presorted else [words[:, u :: 2] for u in range(2)]
 
         def turn(label, sources):
             bank = psum.tile([P, 2 * len(sources), P], F32, name=label, tag=label)
             for g, source in enumerate(sources):
-                words = source[:].bitcast(F32)
                 for u in range(2):
-                    nc.tensor.transpose(bank[:, 2 * g + u, :], words[:, u * P : (u + 1) * P], identity[:])
+                    nc.tensor.transpose(bank[:, 2 * g + u, :], source[u], identity[:])
             return bank
 
         def gather(label, bank):
@@ -219,7 +225,7 @@ def tile_siamese_field_rerank_b12_kernel(
                 in_=live["diff_bank", t, h][:].rearrange("r (p u e) -> r u p e", u=2, e=2),
                 func=ACT.Abs,
             )
-            live["z_sorted", t, h] = z
+            live["z_sorted", t, h] = halves(z)
 
         def turn_z(t, passes=BOTH, bank="z_bank"):
             live["z_bank", t, passes] = turn(bank, [live["z_sorted", t, g] for g in passes])
@@ -273,7 +279,7 @@ def tile_siamese_field_rerank_b12_kernel(
                 out=rounded[:].rearrange("r (u p e) -> r u p e", u=2, e=2),
                 in_=live["y", t][:].rearrange("r (p u e) -> r u p e", u=2, e=2),
             )
-            live["y_sorted", t] = rounded
+            live["y_sorted", t] = halves(rounded)
 
         def turn_y(t, bank="y_bank"):
             live["y_bank", t] = turn(bank, [live["y_sorted", t]])

@@ -25,7 +25,7 @@ TILES = G * TILES_PER_FIELD
 BLOCKS = K // B
 BLOCKS_PER_PASS = PASS // B
 SIDES = 2
-PRESORTED = ((1, 0), (1, 1))
+PRESORTED = ((0, 0), (0, 1), (1, 0), (1, 1))
 BOTH = tuple(range(PASSES))
 
 
@@ -79,6 +79,16 @@ def tile_siamese_field_rerank_b12_kernel(
             for g in range(count):
                 store[first + g] = held[:, g, :]
 
+        spread_bias = {}
+
+        def load_bias(first, count):
+            name = "spread_bias_%d" % first
+            held = keep.tile([P, count * N], BF16, name=name, tag=name)
+            row = bias[first : first + count].rearrange("i c -> (i c)")
+            nc.sync.dma_start(out=held[:], in_=row.partition_broadcast(P))
+            for i in range(count):
+                spread_bias[first + i] = held[:, i * N : (i + 1) * N]
+
         def new_plane(engine, label, count, width):
             plane = keep.tile([P, count, width], U8, name=label, tag=label, align_bytes=64)
             engine.memset(plane[:].bitcast(I32), 0)
@@ -114,28 +124,29 @@ def tile_siamese_field_rerank_b12_kernel(
         load_bytes(1, 1, 1)
         load_bytes(0, 2, 2)
         load_bytes(1, 2, 2)
-        bias_all = keep.tile([P, G * N], BF16, name="bias_all")
-        nc.sync.dma_start(out=bias_all[:], in_=bias.rearrange("i c -> (i c)").partition_broadcast(P))
-        load_plane(w2_plane, w2_scales, 0, G * PASSES)
-        load_words(w2, w2_words, "w2", 0, PASSES)
         rest = TILES - TILES_PER_FIELD
         rest_scale_q = load_row_scales(0, TILES_PER_FIELD, rest)
         rest_scale_d = load_row_scales(1, TILES_PER_FIELD, rest)
+        load_plane(w2_plane, w2_scales, 0, G * PASSES)
+        load_words(w2, w2_words, "w2", 0, PASSES)
         load_bytes(0, TILES_PER_FIELD, TILES_PER_FIELD)
         load_bytes(1, TILES_PER_FIELD, TILES_PER_FIELD)
+        load_bias(0, 1)
         load_plane(w1_plane_rest, w1_scales, PASSES, (G - 1) * PASSES)
         load_words(w1, w1_words, "w1", PASSES, PASSES)
         load_words(w2, w2_words, "w2", PASSES, (G - 1) * PASSES)
+        load_bias(1, G - 1)
         load_bytes(0, 2 * TILES_PER_FIELD, TILES_PER_FIELD)
         load_bytes(1, 2 * TILES_PER_FIELD, TILES_PER_FIELD)
         load_words(w1, w1_words, "w1", 2 * PASSES, PASSES)
-
-        nc.scalar.activation(out=gate_rows[0:TILES, :], in_=prior_rows[:], func=ACT.Sigmoid)
 
         y_codes = keep.tile([P, TILES * P], U32, name="y_codes", align_bytes=64)
         y_plane = keep.tile([P, TILES * P], U8, name="y_plane", align_bytes=64)
         gate = keep.tile([P, TILES], F32, name="gate")
         live = {}
+
+        def squash_prior():
+            nc.scalar.activation(out=gate_rows[0:TILES, :], in_=prior_rows[:], func=ACT.Sigmoid)
 
         def make_gate():
             bank = psum.tile([P, P], F32, name="gate_bank", tag="gate_bank")
@@ -257,7 +268,7 @@ def tile_siamese_field_rerank_b12_kernel(
             field = t // TILES_PER_FIELD
             gated = work.tile([P, N], F32, name="gated_bias", tag="gated_bias", bufs=3)
             nc.scalar.activation(
-                out=gated[:], in_=bias_all[:, field * N : (field + 1) * N], func=ACT.Copy, scale=gate[:, t : t + 1]
+                out=gated[:], in_=spread_bias[field], func=ACT.Copy, scale=gate[:, t : t + 1]
             )
             live["gated_bias", t] = gated
 
@@ -280,6 +291,23 @@ def tile_siamese_field_rerank_b12_kernel(
                 in_=live["y", t][:].rearrange("r (p u e) -> r u p e", u=2, e=2),
             )
             live["y_sorted", t] = halves(rounded)
+
+        def finish_rounded(t):
+            rounded = work.tile([P, N], BF16, name="y_sorted", tag="y_sorted", align_bytes=64)
+            nc.vector.scalar_tensor_tensor(
+                out=rounded[:], in0=live["rel_bank", t][:], scalar=gate[:, t : t + 1], in1=live["gated_bias", t][:],
+                op0=ALU.mult, op1=ALU.add,
+            )
+            words = rounded[:].bitcast(F32)
+            live["y_sorted", t] = [words[:, u :: 2] for u in range(2)]
+
+        def store_plane(first, count, queues):
+            cols = slice(first * P, (first + count) * P)
+            for q in range(4):
+                queues[q % len(queues)].dma_start(
+                    out=out_2[0, 4 * q : 4 * q + 4, cols].bitcast(I32),
+                    in_=y_plane[32 * q : 32 * q + 4, cols].bitcast(I32),
+                )
 
         def turn_y(t, bank="y_bank"):
             live["y_bank", t] = turn(bank, [live["y_sorted", t]])
@@ -308,6 +336,7 @@ def tile_siamese_field_rerank_b12_kernel(
         gather_x(0, 0, (0,))
         gather_x(0, 0, (1,))
         gather_x(0, 1)
+        squash_prior()
         quantize_x(0, 0, (0,))
         quantize_x(0, 0, (1,))
         project(0, 0, 0, (0,))
@@ -318,7 +347,6 @@ def tile_siamese_field_rerank_b12_kernel(
         quantize_x(0, 1)
         widen(1, 0, (1,))
         widen(1, 1)
-        make_gate()
         turn_x(1, 0)
         turn_x(1, 1)
         project(0, 0, 1)
@@ -330,17 +358,18 @@ def tile_siamese_field_rerank_b12_kernel(
         quantize_x(1, 0)
         quantize_x(1, 1)
         absolute(0, 0)
-        gate_bias(0)
+        make_gate()
         use_row_scales(0, TILES_PER_FIELD, rest, rest_scale_q)
 
         last = TILES - 1
         for s in range(1, last):
+            at(widen, s + 2, 0, (0,))
             at(round_y, s - 3)
             at(turn_z, s - 2)
             at(turn_x, s + 1, 0)
             at(turn_x, s + 1, 1)
             at(turn_y, s - 3)
-            at(widen, s + 2, 0)
+            at(widen, s + 2, 0, (1,))
             at(gather_z, s - 2)
             at(absolute, s - 1, 1)
             at(quantize_z, s - 2)
@@ -359,7 +388,7 @@ def tile_siamese_field_rerank_b12_kernel(
             at(project, s, 1, 0)
             at(project, s, 1, 1)
             at(absolute, s, 0)
-            at(gate_bias, s)
+            at(gate_bias, s - 1)
             at(finish, s - 2)
 
         absolute(last - 1, 1)
@@ -371,6 +400,7 @@ def tile_siamese_field_rerank_b12_kernel(
         quantize_z(last - 2)
         gather_z(last - 1)
         quantize_z(last - 1)
+        gate_bias(last - 1)
         gather_y(last - 3)
         quantize_y(last - 3)
         project(last, 0, 0)
@@ -398,16 +428,10 @@ def tile_siamese_field_rerank_b12_kernel(
         gather_y(last - 2)
         quantize_y(last - 2)
         gather_y(last - 1)
-        finish(last)
-        round_y(last)
+        finish_rounded(last)
         quantize_y(last - 1)
+        finish(last)
         turn_y(last)
         gather_y(last)
         quantize_y(last)
-
-        for q in range(4):
-            queue = nc.scalar if q % 2 else nc.sync
-            queue.dma_start(
-                out=out_2[0, 4 * q : 4 * q + 4, :].bitcast(I32),
-                in_=y_plane[32 * q : 32 * q + 4, :].bitcast(I32),
-            )
+        store_plane(0, TILES, (nc.scalar, nc.sync))

@@ -185,7 +185,7 @@ def tile_siamese_field_rerank_b12_kernel(
 
         def gather(label, bank):
             passes = bank.shape[1] // 2
-            grouped = work.tile([P, passes * PASS], BF16, name=label, tag=label, align_bytes=64)
+            grouped = work.tile([P, passes * PASS], BF16, name=label, tag=label, bufs=3, align_bytes=64)
             nc.scalar.copy(
                 out=grouped[:].bitcast(F32).rearrange("p (g r u) -> p g r u", g=passes, u=2),
                 in_=bank[:].rearrange("p (g u) r -> p g r u", u=2),
@@ -210,11 +210,11 @@ def tile_siamese_field_rerank_b12_kernel(
             for g, pair in zip(passes, quantize("x_mx_%d" % side, live["x_grouped", t, side, passes])):
                 live["x_mx", t, side, g] = pair
 
-        def project(t, h, side, passes=BOTH):
+        def project(t, h, side, passes=BOTH, bank=None):
             for g in passes:
                 first = side == 0 and g == 0
                 if first:
-                    name = "diff_bank_%d" % h
+                    name = bank or "diff_bank_%d" % h
                     live["diff_bank", t, h] = psum.tile([P, PASS], F32, name=name, tag=name)
                 codes, plane = live["x_mx", t, side, g]
                 group = t // TILES_PER_FIELD * PASSES + g
@@ -264,19 +264,22 @@ def tile_siamese_field_rerank_b12_kernel(
                     stop=(g == PASSES - 1),
                 )
 
-        def gate_bias(t):
+        def gate_bias(t, on_vector=False):
             field = t // TILES_PER_FIELD
-            gated = work.tile([P, N], F32, name="gated_bias", tag="gated_bias", bufs=3)
-            nc.scalar.activation(
-                out=gated[:], in_=spread_bias[field], func=ACT.Copy, scale=gate[:, t : t + 1]
-            )
+            gated = work.tile([P, N], F32, name="gated_bias", tag="gated_bias", bufs=5)
+            if on_vector:
+                nc.vector.tensor_scalar(
+                    out=gated[:], in0=spread_bias[field], scalar1=gate[:, t : t + 1], scalar2=None, op0=ALU.mult
+                )
+            else:
+                nc.scalar.activation(out=gated[:], in_=spread_bias[field], func=ACT.Copy, scale=gate[:, t : t + 1])
             live["gated_bias", t] = gated
 
         y_rows = out_0.rearrange("i r c -> (i r) c")
         code_rows = out_1[0].rearrange("p m t -> p (m t)").bitcast(I32)
 
         def finish(t):
-            y = work.tile([P, N], F32, name="y", tag="y", bufs=3)
+            y = work.tile([P, N], F32, name="y", tag="y", bufs=4)
             nc.vector.scalar_tensor_tensor(
                 out=y[:], in0=live["rel_bank", t][:], scalar=gate[:, t : t + 1], in1=live["gated_bias", t][:],
                 op0=ALU.mult, op1=ALU.add,
@@ -285,7 +288,7 @@ def tile_siamese_field_rerank_b12_kernel(
             live["y", t] = y
 
         def round_y(t):
-            rounded = work.tile([P, N], BF16, name="y_sorted", tag="y_sorted", align_bytes=64)
+            rounded = work.tile([P, N], BF16, name="y_sorted", tag="y_sorted", bufs=3, align_bytes=64)
             nc.vector.tensor_copy(
                 out=rounded[:].rearrange("r (u p e) -> r u p e", u=2, e=2),
                 in_=live["y", t][:].rearrange("r (p u e) -> r u p e", u=2, e=2),
@@ -293,7 +296,7 @@ def tile_siamese_field_rerank_b12_kernel(
             live["y_sorted", t] = halves(rounded)
 
         def finish_rounded(t):
-            rounded = work.tile([P, N], BF16, name="y_sorted", tag="y_sorted", align_bytes=64)
+            rounded = work.tile([P, N], BF16, name="y_sorted", tag="y_sorted", bufs=3, align_bytes=64)
             nc.vector.scalar_tensor_tensor(
                 out=rounded[:], in0=live["rel_bank", t][:], scalar=gate[:, t : t + 1], in1=live["gated_bias", t][:],
                 op0=ALU.mult, op1=ALU.add,
@@ -363,46 +366,50 @@ def tile_siamese_field_rerank_b12_kernel(
 
         last = TILES - 1
         for s in range(1, last):
-            at(widen, s + 2, 0, (0,))
-            at(round_y, s - 3)
+            at(absolute, s - 1, 1)
             at(turn_z, s - 2)
             at(turn_x, s + 1, 0)
             at(turn_x, s + 1, 1)
-            at(turn_y, s - 3)
-            at(widen, s + 2, 0, (1,))
-            at(gather_z, s - 2)
-            at(absolute, s - 1, 1)
-            at(quantize_z, s - 2)
-            at(gather_x, s + 1, 0)
-            at(gather_x, s + 1, 1)
-            at(gather_y, s - 3)
+            at(turn_y, s - 4)
+            at(widen, s + 2, 0)
             if s + 2 == TILES_PER_FIELD:
                 use_row_scales(1, TILES_PER_FIELD, rest, rest_scale_d)
             at(widen, s + 2, 1)
-            at(quantize_x, s + 1, 0)
-            at(quantize_x, s + 1, 1)
-            at(quantize_y, s - 3)
+            if s + 1 == last:
+                for t in range(s - 2, TILES):
+                    gate_bias(t, True)
+            at(gather_z, s - 2)
+            at(quantize_z, s - 2)
+            at(gather_x, s + 1, 0)
+            at(gather_x, s + 1, 1)
+            at(gather_y, s - 4)
+            at(relevance, s - 3)
             at(project, s, 0, 0)
             at(project, s, 0, 1)
-            at(relevance, s - 2)
             at(project, s, 1, 0)
             at(project, s, 1, 1)
+            if s + 1 < last:
+                at(gate_bias, s - 2)
             at(absolute, s, 0)
-            at(gate_bias, s - 1)
-            at(finish, s - 2)
+            at(finish, s - 3)
+            at(quantize_x, s + 1, 0)
+            at(round_y, s - 3)
+            at(quantize_x, s + 1, 1)
+            at(quantize_y, s - 4)
 
         absolute(last - 1, 1)
-        round_y(last - 3)
+        relevance(last - 3)
         turn_z(last - 2)
-        turn_y(last - 3)
+        turn_y(last - 4)
         turn_z(last - 1, BOTH, "x_bank_0")
         gather_z(last - 2)
+        finish(last - 3)
         quantize_z(last - 2)
         gather_z(last - 1)
+        round_y(last - 3)
         quantize_z(last - 1)
-        gate_bias(last - 1)
-        gather_y(last - 3)
-        quantize_y(last - 3)
+        gather_y(last - 4)
+        quantize_y(last - 4)
         project(last, 0, 0)
         project(last, 0, 1)
         relevance(last - 2)
@@ -410,13 +417,13 @@ def tile_siamese_field_rerank_b12_kernel(
         project(last, 1, 1)
         relevance(last - 1, BOTH, "x_bank_1")
         absolute(last, 0)
-        gate_bias(last)
         finish(last - 2)
         round_y(last - 2)
         absolute(last, 1)
         turn_z(last, (0,))
-        turn_y(last - 2)
+        turn_y(last - 3)
         turn_z(last, (1,), "x_bank_0")
+        turn_y(last - 2, "diff_bank_0")
         finish(last - 1)
         gather_z(last, (0,))
         gather_z(last, (1,))
@@ -425,10 +432,12 @@ def tile_siamese_field_rerank_b12_kernel(
         quantize_z(last, (1,))
         relevance(last)
         turn_y(last - 1, "gate_bank")
+        gather_y(last - 3)
+        quantize_y(last - 3)
         gather_y(last - 2)
+        finish_rounded(last)
         quantize_y(last - 2)
         gather_y(last - 1)
-        finish_rounded(last)
         quantize_y(last - 1)
         finish(last)
         turn_y(last)

from contextlib import ExitStack

import concourse.mybir as mybir
from concourse.masks import make_identity

G, T, K, F, N, B = 3, 512, 1024, 1024, 512, 128
FLOPS = 2 * G * T * (2 * K * F + F * N)

F32 = mybir.dt.float32
BF16 = mybir.dt.bfloat16
I32 = mybir.dt.int32
U32 = mybir.dt.uint32
U8 = mybir.dt.uint8
FP8 = mybir.dt.float8_e4m3fn
FP8X4 = mybir.dt.float8_e4m3fn_x4
FP4X4 = mybir.dt.float4_e2m1fn_x4
ACT = mybir.ActivationFunctionType
ALU = mybir.AluOpType

P = 128
PASS = 512
PASSES = K // PASS
TILES_PER_FIELD = T // P
TILES = G * TILES_PER_FIELD
BLOCKS = K // B
BLOCKS_PER_PASS = PASS // B
SIDES = 2
PRESORTED = ((0, 0), (0, 1), (1, 0), (1, 1))
BOTH = tuple(range(PASSES))


def tile_siamese_field_rerank_b12_kernel(
    tc, xq_bytes, xq_scale, xd_bytes, xd_scale, w1_words, w1_scales, w2_words, w2_scales, bias, prior,
    out_0, out_1, out_2,
):
    nc = tc.nc
    x_bytes = (xq_bytes, xd_bytes)
    x_scale = (xq_scale, xd_scale)

    with ExitStack() as ctx:
        keep = ctx.enter_context(tc.tile_pool(name="keep", bufs=1))
        work = ctx.enter_context(tc.tile_pool(name="work", bufs=2))
        psum = ctx.enter_context(tc.psum_pool(name="psum", bufs=1))
        ctx.enter_context(tc.manual_schedule())

        raw, row_scale, w1, w1_plane, w2 = {}, {}, {}, {}, {}

        def load_bytes(side, first, count):
            name = "fp8_in_%d_%d" % (side, first)
            held = keep.tile([P, count, K], U8, name=name, tag=name)
            rows = x_bytes[side].rearrange("i (j p) k -> p (i j) k", p=P)
            nc.sync.dma_start(out=held[:], in_=rows[:, first : first + count, :])
            for j in range(count):
                raw[side, first + j] = held[:, j, :]

        def load_row_scales(side, first, count):
            name = "row_scale_%d_%d" % (side, first)
            held = keep.tile([P, count, BLOCKS], F32, name=name, tag=name)
            rows = x_scale[side].rearrange("i (j p) b -> p (i j) b", p=P)
            nc.sync.dma_start(out=held[:], in_=rows[:, first : first + count, :])
            return held

        def use_row_scales(side, first, count, held):
            if side == 1:
                name = "negated_scale_%d" % first
                negated = keep.tile([P, count, BLOCKS], F32, name=name, tag=name)
                nc.vector.tensor_scalar(out=negated[:], in0=held[:], scalar1=-1.0, scalar2=None, op0=ALU.mult)
                held = negated
            for j in range(count):
                row_scale[side, first + j] = held[:, j, :]

        def load_words(store, words, label, first, count):
            name = "%s_words_%d" % (label, first)
            held = keep.tile([P, count, words.shape[2]], U8, name=name, tag=name, align_bytes=64)
            nc.sync.dma_start(
                out=held[:].bitcast(I32),
                in_=words[first : first + count].rearrange("g p n -> p g n").bitcast(I32),
            )
            for g in range(count):
                store[first + g] = held[:, g, :]

        spread_bias = {}

        def load_bias(first, count):
            name = "spread_bias_%d" % first
            held = keep.tile([P, count * N], BF16, name=name, tag=name)
            row = bias[first : first + count].rearrange("i c -> (i c)")
            nc.sync.dma_start(out=held[:], in_=row.partition_broadcast(P))
            for i in range(count):
                spread_bias[first + i] = held[:, i * N : (i + 1) * N]

        def new_plane(engine, label, count, width):
            plane = keep.tile([P, count, width], U8, name=label, tag=label, align_bytes=64)
            engine.memset(plane[:].bitcast(I32), 0)
            return plane

        def load_plane(plane, scales, first, count):
            for q in range(4):
                nc.sync.dma_start(
                    out=plane[32 * q : 32 * q + 4, :, :].bitcast(I32),
                    in_=scales[first : first + count, 4 * q : 4 * q + 4, :].rearrange("g r n -> r g n").bitcast(I32),
                )

        prior_rows = keep.tile([TILES, P], BF16, name="prior_rows")
        nc.gpsimd.dma_start(out=prior_rows[:], in_=prior.rearrange("i (j p) -> (i j) p", p=P))
        identity = keep.tile([P, P], F32, name="identity")
        make_identity(nc, identity[:])
        gate_rows = keep.tile([P, P], F32, name="gate_rows")
        nc.gpsimd.memset(gate_rows[:], 0.0)
        w1_plane_first = new_plane(nc.vector, "w1_plane_first", PASSES, F)
        w2_plane = new_plane(nc.vector, "w2_plane", G * PASSES, N)
        w1_plane_rest = new_plane(nc.vector, "w1_plane_rest", (G - 1) * PASSES, F)
        for g in range(G * PASSES):
            w1_plane[g] = w1_plane_first[:, g, :] if g < PASSES else w1_plane_rest[:, g - PASSES, :]

        first_scale_q = load_row_scales(0, 0, TILES_PER_FIELD)
        load_bytes(0, 0, 1)
        first_scale_d = load_row_scales(1, 0, TILES_PER_FIELD)
        load_bytes(1, 0, 1)
        load_plane(w1_plane_first, w1_scales, 0, PASSES)
        load_words(w1, w1_words, "w1", 0, 1)
        load_words(w1, w1_words, "w1", 1, 1)
        load_bytes(0, 1, 1)
        load_bytes(1, 1, 1)
        load_bytes(0, 2, 2)
        load_bytes(1, 2, 2)
        rest = TILES - TILES_PER_FIELD
        rest_scale_q = load_row_scales(0, TILES_PER_FIELD, rest)
        rest_scale_d = load_row_scales(1, TILES_PER_FIELD, rest)
        load_plane(w2_plane, w2_scales, 0, G * PASSES)
        load_words(w2, w2_words, "w2", 0, PASSES)
        load_bytes(0, TILES_PER_FIELD, TILES_PER_FIELD)
        load_bytes(1, TILES_PER_FIELD, TILES_PER_FIELD)
        load_bias(0, 1)
        load_plane(w1_plane_rest, w1_scales, PASSES, (G - 1) * PASSES)
        load_words(w1, w1_words, "w1", PASSES, PASSES)
        load_words(w2, w2_words, "w2", PASSES, (G - 1) * PASSES)
        load_bias(1, G - 1)
        load_bytes(0, 2 * TILES_PER_FIELD, TILES_PER_FIELD)
        load_bytes(1, 2 * TILES_PER_FIELD, TILES_PER_FIELD)
        load_words(w1, w1_words, "w1", 2 * PASSES, PASSES)

        y_codes = keep.tile([P, TILES * P], U32, name="y_codes", align_bytes=64)
        y_plane = keep.tile([P, TILES * P], U8, name="y_plane", align_bytes=64)
        gate = keep.tile([P, TILES], F32, name="gate")
        live = {}

        def squash_prior():
            nc.scalar.activation(out=gate_rows[0:TILES, :], in_=prior_rows[:], func=ACT.Sigmoid)

        def make_gate():
            bank = psum.tile([P, P], F32, name="gate_bank", tag="gate_bank")
            nc.tensor.transpose(bank[:], gate_rows[:], identity[:])
            nc.scalar.copy(out=gate[:], in_=bank[:, 0:TILES])

        def halves(tile):
            words = tile[:].bitcast(F32)
            return [words[:, u * P : (u + 1) * P] for u in range(2)]

        def widen(t, side, passes=BOTH):
            for g in passes:
                name = "x_wide_%d_%d" % (side, g)
                wide = work.tile([P, PASS], BF16, name=name, tag=name, bufs=3, align_bytes=64)
                sorted_view = wide[:].rearrange("r (u q p e) -> r q p u e", u=2, q=BLOCKS_PER_PASS, e=2)
                presorted = (side, g) in PRESORTED
                for q in range(BLOCKS_PER_PASS):
                    b = g * BLOCKS_PER_PASS + q
                    codes = raw[side, t][:, b * B : (b + 1) * B].bitcast(FP8)
                    nc.vector.tensor_scalar(
                        out=sorted_view[:, q] if presorted else wide[:, q * B : (q + 1) * B],
                        in0=codes.rearrange("r (p u e) -> r p u e", u=2, e=2) if presorted else codes,
                        scalar1=row_scale[side, t][:, b : b + 1],
                        scalar2=None,
                        op0=ALU.mult,
                    )
                words = wide[:].bitcast(F32)
                live["x_wide", t, side, g] = halves(wide) if presorted else [words[:, u :: 2] for u in range(2)]

        def turn(label, sources):
            bank = psum.tile([P, 2 * len(sources), P], F32, name=label, tag=label)
            for g, source in enumerate(sources):
                for u in range(2):
                    nc.tensor.transpose(bank[:, 2 * g + u, :], source[u], identity[:])
            return bank

        def gather(label, bank):
            passes = bank.shape[1] // 2
            grouped = work.tile([P, passes * PASS], BF16, name=label, tag=label, bufs=3, align_bytes=64)
            nc.scalar.copy(
                out=grouped[:].bitcast(F32).rearrange("p (g r u) -> p g r u", g=passes, u=2),
                in_=bank[:].rearrange("p (g u) r -> p g r u", u=2),
            )
            return grouped

        def quantize(label, grouped):
            passes = grouped.shape[1] // PASS
            codes = work.tile([P, passes * P], U32, name=label + "_codes", tag=label + "_codes", bufs=3, align_bytes=64)
            plane = work.tile([P, passes * P], U8, name=label + "_plane", tag=label + "_plane", bufs=3, align_bytes=64)
            nc.vector.quantize_mx(out=codes[:].bitcast(FP8X4), scales=plane[:], in_=grouped[:])
            return [(codes[:, g * P : (g + 1) * P], plane[:, g * P : (g + 1) * P]) for g in range(passes)]

        def turn_x(t, side, passes=BOTH, bank=None):
            sources = [live["x_wide", t, side, g] for g in passes]
            live["x_bank", t, side, passes] = turn(bank or "x_bank_%d" % side, sources)

        def gather_x(t, side, passes=BOTH):
            live["x_grouped", t, side, passes] = gather("x_grouped_%d" % side, live["x_bank", t, side, passes])

        def quantize_x(t, side, passes=BOTH):
            for g, pair in zip(passes, quantize("x_mx_%d" % side, live["x_grouped", t, side, passes])):
                live["x_mx", t, side, g] = pair

        def project(t, h, side, passes=BOTH, bank=None):
            for g in passes:
                first = side == 0 and g == 0
                if first:
                    name = bank or "diff_bank_%d" % h
                    live["diff_bank", t, h] = psum.tile([P, PASS], F32, name=name, tag=name)
                codes, plane = live["x_mx", t, side, g]
                group = t // TILES_PER_FIELD * PASSES + g
                nc.tensor.matmul_mx(
                    out=live["diff_bank", t, h][:],
                    lhsT=codes.bitcast(FP8X4),
                    lhsT_scale=plane,
                    rhs=w1[group][:, 2 * h * PASS : 2 * (h + 1) * PASS].bitcast(FP4X4),
                    rhs_scale=w1_plane[group][:, h * PASS : (h + 1) * PASS],
                    start=first,
                    stop=(side == SIDES - 1 and g == PASSES - 1),
                )

        def absolute(t, h):
            name = "z_sorted_%d" % h
            z = work.tile([P, PASS], BF16, name=name, tag=name, bufs=3, align_bytes=64)
            nc.scalar.activation(
                out=z[:].rearrange("r (u p e) -> r u p e", u=2, e=2),
                in_=live["diff_bank", t, h][:].rearrange("r (p u e) -> r u p e", u=2, e=2),
                func=ACT.Abs,
            )
            live["z_sorted", t, h] = halves(z)

        def turn_z(t, passes=BOTH, bank="z_bank"):
            live["z_bank", t, passes] = turn(bank, [live["z_sorted", t, g] for g in passes])

        def gather_z(t, passes=BOTH):
            live["z_grouped", t, passes] = gather("z_grouped", live["z_bank", t, passes])

        def quantize_z(t, passes=BOTH):
            for g, pair in zip(passes, quantize("z_mx", live["z_grouped", t, passes])):
                live["z_mx", t, g] = pair

        def relevance(t, passes=BOTH, bank="rel_bank"):
            for g in passes:
                if g == 0:
                    live["rel_bank", t] = psum.tile([P, N], F32, name=bank, tag=bank)
                codes, plane = live["z_mx", t, g]
                group = t // TILES_PER_FIELD * PASSES + g
                nc.tensor.matmul_mx(
                    out=live["rel_bank", t][:],
                    lhsT=codes.bitcast(FP8X4),
                    lhsT_scale=plane,
                    rhs=w2[group].bitcast(FP4X4),
                    rhs_scale=w2_plane[:, group, :],
                    start=(g == 0),
                    stop=(g == PASSES - 1),
                )

        def gate_bias(t, on_vector=False):
            field = t // TILES_PER_FIELD
            gated = work.tile([P, N], F32, name="gated_bias", tag="gated_bias", bufs=5)
            if on_vector:
                nc.vector.tensor_scalar(
                    out=gated[:], in0=spread_bias[field], scalar1=gate[:, t : t + 1], scalar2=None, op0=ALU.mult
                )
            else:
                nc.scalar.activation(out=gated[:], in_=spread_bias[field], func=ACT.Copy, scale=gate[:, t : t + 1])
            live["gated_bias", t] = gated

        y_rows = out_0.rearrange("i r c -> (i r) c")
        code_rows = out_1[0].rearrange("p m t -> p (m t)").bitcast(I32)

        def finish(t):
            y = work.tile([P, N], F32, name="y", tag="y", bufs=4)
            nc.vector.scalar_tensor_tensor(
                out=y[:], in0=live["rel_bank", t][:], scalar=gate[:, t : t + 1], in1=live["gated_bias", t][:],
                op0=ALU.mult, op1=ALU.add,
            )
            nc.sync.dma_start(out=y_rows[t * P : (t + 1) * P, :], in_=y[:])
            live["y", t] = y

        def round_y(t):
            rounded = work.tile([P, N], BF16, name="y_sorted", tag="y_sorted", bufs=3, align_bytes=64)
            nc.vector.tensor_copy(
                out=rounded[:].rearrange("r (u p e) -> r u p e", u=2, e=2),
                in_=live["y", t][:].rearrange("r (p u e) -> r u p e", u=2, e=2),
            )
            live["y_sorted", t] = halves(rounded)

        def finish_rounded(t):
            rounded = work.tile([P, N], BF16, name="y_sorted", tag="y_sorted", bufs=3, align_bytes=64)
            nc.vector.scalar_tensor_tensor(
                out=rounded[:], in0=live["rel_bank", t][:], scalar=gate[:, t : t + 1], in1=live["gated_bias", t][:],
                op0=ALU.mult, op1=ALU.add,
            )
            words = rounded[:].bitcast(F32)
            live["y_sorted", t] = [words[:, u :: 2] for u in range(2)]

        def store_plane(first, count, queues):
            cols = slice(first * P, (first + count) * P)
            for q in range(4):
                queues[q % len(queues)].dma_start(
                    out=out_2[0, 4 * q : 4 * q + 4, cols].bitcast(I32),
                    in_=y_plane[32 * q : 32 * q + 4, cols].bitcast(I32),
                )

        def turn_y(t, bank="y_bank"):
            live["y_bank", t] = turn(bank, [live["y_sorted", t]])

        def gather_y(t):
            live["y_grouped", t] = gather("y_grouped", live["y_bank", t])

        def quantize_y(t):
            cols = slice(t * P, (t + 1) * P)
            nc.vector.quantize_mx(
                out=y_codes[:, cols].bitcast(FP8X4), scales=y_plane[:, cols], in_=live["y_grouped", t][:]
            )
            nc.sync.dma_start(out=code_rows[:, cols], in_=y_codes[:, cols].bitcast(I32))

        def at(stage, t, *more):
            if 0 <= t < TILES:
                stage(t, *more)

        use_row_scales(0, 0, TILES_PER_FIELD, first_scale_q)
        widen(0, 0)
        use_row_scales(1, 0, TILES_PER_FIELD, first_scale_d)
        widen(0, 1)
        turn_x(0, 0, (0,))
        turn_x(0, 0, (1,), "z_bank")
        turn_x(0, 1)
        gather_x(0, 0, (0,))
        gather_x(0, 0, (1,))
        gather_x(0, 1)
        squash_prior()
        quantize_x(0, 0, (0,))
        quantize_x(0, 0, (1,))
        project(0, 0, 0, (0,))
        project(0, 1, 0, (0,))
        project(0, 0, 0, (1,))
        project(0, 1, 0, (1,))
        widen(1, 0, (0,))
        quantize_x(0, 1)
        widen(1, 0, (1,))
        widen(1, 1)
        turn_x(1, 0)
        turn_x(1, 1)
        project(0, 0, 1)
        project(0, 1, 1)
        gather_x(1, 0)
        gather_x(1, 1)
        widen(2, 0)
        widen(2, 1)
        quantize_x(1, 0)
        quantize_x(1, 1)
        absolute(0, 0)
        make_gate()
        use_row_scales(0, TILES_PER_FIELD, rest, rest_scale_q)

        last = TILES - 1
        for s in range(1, last):
            at(absolute, s - 1, 1)
            at(turn_z, s - 2)
            at(turn_x, s + 1, 0)
            at(turn_x, s + 1, 1)
            at(turn_y, s - 4)
            at(widen, s + 2, 0)
            if s + 2 == TILES_PER_FIELD:
                use_row_scales(1, TILES_PER_FIELD, rest, rest_scale_d)
            at(widen, s + 2, 1)
            if s + 1 == last:
                for t in range(s - 2, TILES):
                    gate_bias(t, True)
            at(gather_z, s - 2)
            at(quantize_z, s - 2)
            at(gather_x, s + 1, 0)
            at(gather_x, s + 1, 1)
            at(gather_y, s - 4)
            at(relevance, s - 3)
            at(project, s, 0, 0)
            at(project, s, 0, 1)
            at(project, s, 1, 0)
            at(project, s, 1, 1)
            if s + 1 < last:
                at(gate_bias, s - 2)
            at(absolute, s, 0)
            at(finish, s - 3)
            at(quantize_x, s + 1, 0)
            at(round_y, s - 3)
            at(quantize_x, s + 1, 1)
            at(quantize_y, s - 4)

        absolute(last - 1, 1)
        relevance(last - 3)
        turn_z(last - 2)
        turn_y(last - 4)
        turn_z(last - 1, BOTH, "x_bank_0")
        gather_z(last - 2)
        finish(last - 3)
        quantize_z(last - 2)
        gather_z(last - 1)
        round_y(last - 3)
        quantize_z(last - 1)
        gather_y(last - 4)
        quantize_y(last - 4)
        project(last, 0, 0)
        project(last, 0, 1)
        relevance(last - 2)
        project(last, 1, 0)
        project(last, 1, 1)
        relevance(last - 1, BOTH, "x_bank_1")
        absolute(last, 0)
        finish(last - 2)
        round_y(last - 2)
        absolute(last, 1)
        turn_z(last, (0,))
        turn_y(last - 3)
        turn_z(last, (1,), "x_bank_0")
        turn_y(last - 2, "diff_bank_0")
        finish(last - 1)
        gather_z(last, (0,))
        gather_z(last, (1,))
        quantize_z(last, (0,))
        round_y(last - 1)
        quantize_z(last, (1,))
        relevance(last)
        turn_y(last - 1, "gate_bank")
        gather_y(last - 3)
        quantize_y(last - 3)
        gather_y(last - 2)
        finish_rounded(last)
        quantize_y(last - 2)
        gather_y(last - 1)
        quantize_y(last - 1)
        finish(last)
        turn_y(last)
        gather_y(last)
        quantize_y(last)
        store_plane(0, TILES, (nc.scalar, nc.sync))
